import numpy as np, ml_dtypes
CORES = [3,7,11,15,131,135,139,143]
N = 8
BF = ml_dtypes.bfloat16
def f(rng, *shape):
    return (rng.standard_normal(shape, dtype=np.float32) * np.exp2(rng.integers(-2, 3, shape[:-1] + (1,)))).astype(BF)
def wide(rng, *shape):
    v = f(rng, *shape).astype(np.float32); k = shape[:-2] + (1, shape[-1])
    return (v * np.exp2(rng.integers(-6, 7, k)) * (rng.random(k) > 0.0625)).astype(BF)
def gentries(a):
    return np.ascontiguousarray(a.reshape(8, 16, -1).transpose(0, 2, 1)).reshape(8, -1)
def gtable(e):
    e = np.asarray(e); return np.ascontiguousarray(e.reshape(8, -1, 16).transpose(0, 2, 1)).reshape(128, -1).astype(np.int32)
NV, NC, E, B, CX, A, KN = 2048, 512, 1536, 64, 32, 112, 8
def lists8(a):
    return np.stack([gentries(v) for v in a])
def tables8(e):
    return np.stack([gtable(v) for v in e])
def cases(s, cor):
    t = np.take_along_axis(s, lists8(cor), -1).reshape(N, 8, 8, NC).astype(np.int64)
    return np.sum(t << np.arange(8)[:, None], axis=2)
def crossings(s, bl):
    w = np.take_along_axis(s, lists8(bl), -1).reshape(N, 8, N, B).transpose(0, 2, 1, 3)
    return w != w.transpose(1, 0, 2, 3)
def pick(rng, s, want, h):
    o = np.argsort(s, axis=-1, kind="stable"); n0 = NV - np.sum(s, axis=-1, keepdims=True)
    u = rng.integers(0, 4, want.shape) * 0.25 if h else rng.random(want.shape)
    i = np.where(want, n0 + np.minimum(np.floor(u * (NV - n0)), NV - n0 - 1), np.minimum(np.floor(u * n0), n0 - 1)).astype(np.int64)
    return np.take_along_axis(o, i, -1)
def make(rng, act, cross, zero=0.0625, h=False):
    s = rng.random((N, 8, NV)) < rng.uniform(0.3, 0.7, (N, 8, 1))
    m = (rng.random(s.shape) + 0.0625) * np.exp2(rng.integers(-3, 4, s.shape))
    z = np.where(rng.random(s.shape) < 0.5, 0.0, -0.0)
    lv = np.where(s, -m, np.where(rng.random(s.shape) < zero, z, m)).astype(BF)
    key = rng.random((N, 8, NC)); key[..., 0] -= rng.integers(0, 2, (N, 8)); key[..., -1] -= rng.integers(0, 2, (N, 8))
    on = (np.argsort(np.argsort(key, axis=-1), axis=-1) < act[..., None])[:, :, None]
    k = np.arange(8)[:, None]; c1 = rng.integers(0, 8, (N, 8, 1, NC)); c2 = (c1 + rng.integers(1, 8, c1.shape)) % 8
    w = (rng.random((N, 8, 8, NC)) < 0.5) & (k != c2) | (k == c1)
    w = np.where(on, w, rng.random((N, 8, 1, NC)) < 0.5)
    wa = rng.random((N, 8, E)) < 0.5; x = rng.random((N, 8, E)) < 0.75; x[..., 0] = True; x[..., -1] = True
    wb = wa ^ x
    c = np.argsort(rng.random((N, N, 8, B)), axis=-1) < cross[..., None]
    b = rng.random((N, N, 8, B)) < 0.5
    for q in range(N):
        for r in range(q + 1, N): b[r, q] = b[q, r] ^ c[q, r]
    tab = rng.integers(0, 12, (N, 16, 256 * KN)); tab[rng.random(tab.shape) < 0.2] = -1
    return {"lv": lv, "ch": f(rng, N, 128, NV), "cor": tables8(pick(rng, s, w.reshape(N, 8, 8 * NC), h)), "kd": rng.integers(0, KN, (N, 8, NC)).astype(np.int32),
            "ce": rng.integers(0, E + N * B, (N, 8, 12 * NC)).astype(np.int32), "ea": tables8(pick(rng, s, wa, h)), "eb": tables8(pick(rng, s, wb, h)),
            "bl": tables8(pick(rng, s, b.transpose(0, 2, 1, 3).reshape(N, 8, N * B), h)), "tab": tab.astype(np.int32)}
def sizes(rng):
    act = rng.integers(A >> 1, A + 1, (N, 8)); act[rng.integers(0, N), rng.integers(0, 8)] = A
    cross = rng.integers(CX >> 1, CX + 1, (N, N, 8)); q, r = np.sort(rng.choice(N, 2, replace=False)); cross[q, r, rng.integers(0, 8)] = CX
    return act, cross
def setup_inputs(rng):
    return make(rng, *sizes(rng))
def setup_inputs_full(rng):
    return make(rng, np.full((N, 8), A), np.full((N, N, 8), CX))
def setup_inputs_few(rng):
    act = rng.choice(np.array([0, 1, A >> 2]), (N, 8)); act[np.arange(N), rng.integers(0, 8, N)] = A >> 2
    return make(rng, act, rng.choice(np.array([0, 1, CX]), (N, N, 8)))
def setup_inputs_zeros(rng):
    d = make(rng, *sizes(rng), zero=0.5); tab = d["tab"]; w = rng.integers(0, 6, (N, 1, 256 * KN)); e = rng.integers(0, 12, w.shape).astype(np.int32)
    tab = np.where(w == 0, -1, np.where(w == 1, e, tab)); tab = np.where((w == 2) & (np.arange(16)[:, None] < 15), -1, np.where(w == 2, e, tab))
    d["tab"] = tab.astype(np.int32); return d
def setup_inputs_alike(rng):
    d = make(rng, *sizes(rng), h=True); p = rng.integers(0, E + N * B, (N, 8, 8)); p[..., 0] = 0; p[..., 1] = E + N * B - 1
    d["ce"] = np.take_along_axis(p, rng.integers(0, 8, (N, 8, 12 * NC)), -1).astype(np.int32)
    d["kd"] = np.repeat(rng.integers(0, KN, (N, 8, 1)), NC, axis=-1).astype(np.int32); return d
def setup_inputs_spread(rng):
    d = setup_inputs(rng); d["ch"] = wide(rng, N, 128, NV)
    d["lv"] = (d["lv"].astype(np.float32) * np.exp2(rng.integers(-6, 7, d["lv"].shape))).astype(BF); return d
def check_inputs(d):
    bad = [a for a, lo, hi in (("cor", 0, NV - 1), ("kd", 0, KN - 1), ("ce", 0, E + N * B - 1), ("ea", 0, NV - 1), ("eb", 0, NV - 1), ("bl", 0, NV - 1), ("tab", -1, 11)) if d[a].min() < lo or d[a].max() > hi]
    bad += [a for a in ("lv", "ch") if not np.isfinite(d[a].astype(np.float32)).all()]
    if bad: return bad
    s = d["lv"].astype(np.float32) < 0; c = cases(s, d["cor"])
    if np.sum((c > 0) & (c < 255), axis=-1).max() > A: bad.append("active cells")
    if np.sum(crossings(s, d["bl"]), axis=-1).max() > CX: bad.append("crossing border edges")
    return bad
def reference(lv, ch, cor, kd, ce, ea, eb, bl, tab):
    y = np.zeros((N, 128, 16 * A), np.float32); zero = np.float32(0)
    s = lv.astype(np.float32) < 0; c = ch.astype(np.float32).reshape(N, 8, 16, NV)
    case = cases(s, cor); cross = crossings(s, bl); la, lb, lx = lists8(ea), lists8(eb), lists8(bl).reshape(N, 8, N, B)
    for r in range(N):
        for g in range(8):
            v = np.zeros((16, E + N * B), np.float32); i, j = la[r, g], lb[r, g]
            v[:, :E] = np.where(s[r, g][i] != s[r, g][j], c[r, g][:, i] + c[r, g][:, j], zero)
            for q in range(N):
                v[:, E + q * B:E + (q + 1) * B] = np.where(cross[r, q, g], c[r, g][:, lx[r, g, q]] + c[q, g][:, lx[q, g, r]], zero)
            m = np.flatnonzero((case[r, g] > 0) & (case[r, g] < 255))
            e = tab[r][:, 256 * kd[r, g, m] + case[r, g, m]].T
            n = ce[r, g][12 * m[:, None] + np.maximum(e, 0)].reshape(-1)
            y[r, 16 * g:16 * g + 16, :16 * len(m)] = np.where(e.reshape(-1) >= 0, v[:, n], zero)
    return {"y": y}

@@ -1,0 +1,380 @@
+from concourse.bass import DstId, RemoteDMATransfer, IndirectOffsetOnAxis
+from concourse.mybir import AluOpType, ActivationFunctionType
+
+NV, NC, E, B, A, N = 2048, 512, 1536, 64, 112, 8
+Z = E + N * B
+PAD = 16
+BIG = 4096.0
+VDEF = float(32 * Z + 1)
+EC = 3
+EW = 96 // EC
+CFG = {
+    "out": (14, 16, 14, 12),
+    "V": "consts o_cor c1a c0b c0a prm o_l snd_s c1b cey kd cez case kdw case2 case3 cet slot0 abf x0 case4 slot1 tabg "
+         "x1 slot2 z0 scat z1 x2 scat1 z2 u0 u1 xb0 xb1 u2 vb out",
+    "S": "cor bl lv ea ce0 c3a c2b c2a snd_c c3b eb0 ea0 eb1 ea1 ea2 eb2 xa0 xa1 xa2 xb2 cb s out",
+    "P": "c2 c0 c3 c1 l e0 e1 x0 x1 e2 x2 b u s",
+    "Y": "kd1 eb ch kd0 ce1 out",
+    "G": "zer one p wd cf w park tab w2 send idf b m16 end",
+}
+
+F32, BF, I32, U16 = "float32", "bfloat16", "int32", "uint16"
+SCRATCH = {k: ("psum", [128, 512], F32) for k in ("pc", "pe0", "pe1", "pe2", "pl", "pbd", "pbs", "ps")}
+for _dt, _bufs in (
+        (BF, dict(lvw=[NV], chw=[NV + 2 * PAD], gl=[7168], zer=[144], one=[128], wd=[144], idb=[128], bc=[128], nbc=[128],
+                  t1=[128], t2=[128], t3=[128], hi=[128], w1=[128], bi=[128], pat=[256], aa=[68], se=[192], xa=[E],
+                  xs=[16 * EW], sendb=[2 * B * N], land=[2 * B * N])),
+        (I32, dict(tabw=[2048], lst=[480], cex=[2, 16, 12], kdx=[32], pi=[4], ti=[4])),
+        (U16, dict(off=[480], prm=[32], colu=[32], su=[32], eu=[A], o2u=[A], oabu=[192])),
+        (F32, dict(abf=[192], cey=[32, 16], cez=[NC], cet=[NC], kdf=[32], kdw=[32], pf=[4], cf=[32], idf=[128], park=[32],
+                   m16=[A], n16=[32], cs=[256], colf=[32], lf=[32], lm=[32], tabg=[NC], vw=[768], ef=[A], vt=[Z + 16],
+                   ww=[16 * A], yo=[16 * A], cb=[B * N]))):
+    for _k, _sh in _bufs.items():
+        SCRATCH[_k] = ("sbuf", [128] + _sh, _dt)
+SEMAPHORES = ["arr", "sent"] + ["s%d" % i for i in range(100)]
+
+
+def exchange_calls(core, T, topo):
+    near = [c for c in T.cores if c != core and c in topo.cores_of(core)]
+    far = [c for c in T.cores if c != core and c not in near]
+    me = T.rank_of(core)
+    far.sort(key=lambda c: (T.rank_of(c) - me) % N)
+    out = topo.engines(core, far[0])
+    first, second = far[:len(out) // 2], far[len(out) // 2:]
+    call1 = [(c, out[2 * i:2 * i + 2]) for i, c in enumerate(first)]
+    w = len(out) // len(second)
+    call2 = [(c, out[w * i:w * i + w]) for i, c in enumerate(second)]
+    for c in near:
+        call1.append((c, [e for e in topo.engines(core, c) if e not in out][0:4:2]))
+    return [call1, call2]
+
+
+def rank_program(g, core, T, topo):
+    r = T.rank_of(core)
+    if r is None:
+        return
+    op = AluOpType
+    act = ActivationFunctionType
+    V, S, P = g.vector, g.scalar, g.tensor
+    eng = {"V": V, "S": S, "P": P, "Y": g.sync, "G": g}
+    parts = {q: {} for q in eng}
+    here = [""]
+    on_s = CFG["S"].split()
+
+    def part(name):
+        here[0] = name
+
+    def who():
+        return "S" if here[0] in on_s else "V"
+
+    def add(q, sig, waits, fn, inc=1):
+        parts[q].setdefault(here[0], []).append((sig, list(waits), fn, inc))
+
+    def dma(q, sig, waits, out, in_):
+        add(q, sig, waits, lambda: eng[q].dma_start(out, in_), 16)
+
+    def load(name, sig, waits, out, in_):
+        part(name)
+        dma("S" if name in on_s else "Y", sig, waits, out, in_)
+
+    def ts(sig, waits, out, in0, s1, o0, s2=None, o1=None):
+        if o1 is None:
+            add("V", sig, waits, lambda: V.tensor_scalar(out, in0, s1, None, o0))
+        else:
+            add("V", sig, waits, lambda: V.tensor_scalar(out, in0, s1, s2, o0, o1))
+
+    def tt(sig, waits, out, in0, in1, o):
+        add("V", sig, waits, lambda: V.tensor_tensor(out, in0, in1, o))
+
+    def fill(sig, waits, out, c):
+        add("V", sig, waits, lambda: V.memset(out, c))
+
+    def copy(q, sig, waits, out, in_):
+        if q == "V":
+            add(q, sig, waits, lambda: V.tensor_copy(out, in_))
+        else:
+            add(q, sig, waits, lambda: S.activation(out, in_, act.Copy))
+
+    def sign(sig, waits, out, in_):
+        if who() == "S":
+            add("S", sig, waits, lambda: S.activation(out, in_, act.Sign, bias=2.0 ** -120, scale=2.0 ** 16))
+        else:
+            ts(sig, waits, out, in_, 0.0, op.is_lt, -2.0, op.mult)
+
+    def mm(sig, waits, out, pairs):
+        for i, (lhs, rhs) in enumerate(pairs):
+            last = i == len(pairs) - 1
+            add("P", sig if last else None, waits if i == 0 else [],
+                lambda lhs=lhs, rhs=rhs, i=i, last=last: P.matmul(out, lhs, rhs, i == 0, last))
+
+    def unwrap(sig, waits, out, c0, n):
+        mm(sig, waits, out, [(T.wd[:, 15 - t:143 - t], T.gl[:, 16 * c0 + t:16 * (c0 + n):16]) for t in range(16)])
+
+    def iota(sig, out, pattern, base, cm):
+        add("G", sig, [], lambda: g.iota(out, pattern, base, cm, allow_small_or_imprecise_dtypes=True))
+
+    def pick(sig, waits, out, in_, pattern, cmp, val, base, cm):
+        add("G", sig, waits, lambda: g.affine_select(out, in_, pattern, cmp, val, base, cm))
+
+    def levels(c0, n):
+        return T.lvw[:, 0:NV].indirect(T.off[:, c0:c0 + n])
+
+    def channels(c0):
+        return T.chw[:, 0:NV + 2 * PAD].indirect(T.oabu[:, c0:c0 + EW])
+
+    lift = sum(8.5 * 2 ** kp for kp in range(4) if "c%da" % kp in on_s)
+
+    load("cor", "d_cor", [], T.lst[:, 0:256], T.cor[:])
+    load("bl", "d_bl", [], T.lst[:, 448:480], T.bl[:])
+    load("kd0", "d_kd", [], T.kdx[:, 0:16], T.kd[0::2, :])
+    load("kd1", "d_kd", [], T.kdx[:, 16:32], T.kd[1::2, :])
+    load("lv", "d_lv", ["lvz"], T.lvw[0::16, :], T.lv[:])
+    load("ea", "d_l", ["lvz"], T.lst[:, 256:352], T.ea[:])
+    load("eb", "d_l", ["lvz"], T.lst[:, 352:448], T.eb[:])
+    load("ce0", "d_ce", [], T.cex[:, 0], T.ce[0::2, :])
+    load("ce1", "d_ce", [], T.cex[:, 1], T.ce[1::2, :])
+    load("ch", "d_ch", [], T.chw[:, PAD:PAD + NV], T.ch[:])
+    part("tab")
+    add("G", "d_tab", ["c_t"], lambda: g.indirect_dma_start(
+        T.tabw[:], None, T.tab[:], IndirectOffsetOnAxis(ap=T.ti[:, 0:1], axis=0), bounds_check=15), 16)
+
+    diag, blocks = [[1, 128]], [[16, 8], [0, 16]]
+    part("p")
+    add("G", "i_p", [], lambda: g.iota(T.pi[:, 0:1], [[0, 1]], 0, 1))
+    part("zer")
+    iota("zer", T.zer[:], [[0, 144]], 0, 0)
+    part("one")
+    iota("one", T.one[:], [[0, 128]], 1, 0)
+    part("cf")
+    iota("i_cf", T.cf[:], [[1, 32]], 0, 0)
+    part("park")
+    iota("i_park", T.park[:], [[16, 32]], A, 1)
+    part("wd")
+    pick("c_wd", ["zer"], T.wd[:], T.zer[:], [[16, 9], [-200, 16]], op.not_equal, -0.5, 3000, -1)
+    part("w")
+    pick("t1", ["one"], T.t1[:], T.one[:], diag, op.is_gt, 0.0, 0, -1)
+    pick("t2", [], T.t2[:], T.one[:], [[-1, 128]], op.is_ge, 0.0, 0, 1)
+    pick("t3", ["t1"], T.t3[:], T.t1[:], [[-16, 8], [0, 16]], op.is_ge, 0.0, 0, 1)
+    part("w2")
+    pick("c_w", ["t2"], T.hi[:], T.t2[:], blocks, op.is_ge, 0.0, 15, -1)
+    pick("c_w", ["t3"], T.w1[:], T.t3[:], diag, op.not_equal, -BIG, 0, -1)
+    pick("c_w", ["zer"], T.bi[:], T.zer[:, 0:128], diag, op.not_equal, BIG, 0, -1)
+    part("idf")
+    pick("c_idf", ["zer"], T.idf[:], T.zer[:, 0:128], diag, op.not_equal, 1.0, 0, -1)
+    part("b")
+    pick("c_b", ["zer"], T.idb[:], T.zer[:, 0:128], diag, op.not_equal, 1.0, 0, -1)
+    pick("c_b", [], T.bc[:], T.zer[:, 0:128], blocks, op.not_equal, 1.0, 0, -1)
+    pick("c_b", [], T.nbc[:], T.zer[:, 0:128], blocks, op.not_equal, -1.0, 0, -1)
+    part("m16")
+    pieces, m0 = [], 0
+    for n in CFG["out"]:
+        iota("i_m16", T.m16[:, m0:m0 + 2 * n], [[0, 2], [16, n]], 0, 0)
+        pieces.append((m0, n))
+        m0 += 2 * n
+
+    part("consts")
+    fill("lvz", [], T.lvw[:], 0.0)
+    ts("c_t", ["i_p"], T.ti[:, 0:1], T.pi[:, 0:1], 15, op.bitwise_and)
+    fill("pat2", [], T.pat[:], 2.0)
+    ts("c_t32", ["c_t"], T.pf[:, 0:1], T.ti[:, 0:1], 32.0, op.mult)
+    fill("c_pat", ["pat2"], T.pat[:, 0::8], 0.0)
+    fill("c_cey", [], T.cey[:, :, 0:1], VDEF)
+    fill("c_cey", [], T.cey[:, :, 13:16], VDEF)
+    fill("c_chz", [], T.chw[:, 0:PAD], 0.0)
+    fill("c_chz", [], T.chw[:, PAD + NV:], 0.0)
+    fill("vt", [], T.vt[:, Z:Z + 16], 0.0)
+    fill("vt", [], T.vt[:, E + B * r:E + B * r + B], 0.0)
+    fill("c_vw", [], T.vw[:, 0:A], VDEF)
+    fill("c_a", [], T.aa[:, 1::34], 0.5)
+    fill("c_n16", [], T.n16[:], -16.0)
+    part("o_cor")
+    copy("V", "o_cor", ["d_cor"], T.off[:, 0:256:2], T.lst[:, 128:256])
+    copy("V", "o_cor", [], T.off[:, 1:256:2], T.lst[:, 0:128])
+    copy("V", "o_bl", ["d_bl"], T.off[:, 448:480], T.lst[:, 448:480])
+    part("o_l")
+    copy("V", "o_l", ["d_l"], T.off[:, 256:448], T.lst[:, 256:448])
+    part("abf")
+    ts("abf", ["d_l"], T.abf[:], T.lst[:, 256:448], PAD - BIG, op.add)
+    part("kd")
+    ts("kdf", ["d_kd"], T.kdf[:], T.kdx[:], 256.0, op.mult, lift, op.add)
+    part("prm")
+    ts("c_prm", ["c_t32", "i_cf"], T.prm[:], T.cf[:], T.pf[:, 0:1], op.add)
+
+    part("cey")
+    for k in range(2):
+        ts("cey", ["d_ce"], T.cey[:, k::2, 1:13], T.cex[:, k], 32.0, op.mult, 1.0, op.add)
+    part("kdw")
+    add("V", "kdw", ["kdf"], lambda: V.transpose(T.kdw[:], T.kdf[:]))
+    part("cez")
+    add("V", "cez", ["cey", "c_cey"], lambda: V.transpose(T.cez[:], T.cey[:]))
+    part("cet")
+    copy(who(), "cet", ["cez", "c_prm"], T.cet[:], T.cez[:, 0:NC].indirect(T.prm[:, 0:32]))
+
+    for kp in range(4):
+        for h in range(2):
+            part("c%d%s" % (kp, "ab"[h]))
+            assert (who() == "S") == ("c%da" % kp in on_s)
+            c0 = 64 * kp + 32 * h
+            sign("g_c%d" % kp, ["d_lv", "o_cor"], T.gl[:, 16 * c0:16 * (c0 + 32)], levels(c0, 32))
+        part("c%d" % kp)
+        unwrap("p_c", ["g_c%d" % kp, "c_wd"], T.pc[:, 3 - kp:256:4], 64 * kp, 64)
+
+    part("snd_s")
+    sign("snd", ["o_bl", "d_lv"], T.sendb[:, 1::2], levels(448, 32))
+    part("snd_c")
+    copy(who(), "snd", ["o_bl", "d_ch"], T.sendb[:, 0::2], T.chw[:, PAD:PAD + NV].indirect(T.off[:, 448:480]))
+    part("send")
+    sent = 0
+    for call in exchange_calls(core, T, topo):
+        trs = []
+        for c, es in call:
+            rid, pid = topo.addr(c, core)
+            q = T.rank_of(c)
+            trs.append(RemoteDMATransfer(dst_ids=[DstId(rid=rid, pnc=pid)], dma_engine_mask=sum(1 << e for e in es),
+                                         remote_sem=T.sem.arr, src=T.sendb[:, 2 * B * q:2 * B * (q + 1)],
+                                         dst=T.land[:, 2 * B * r:2 * B * (r + 1)]))
+            sent += len(es)
+        add("G", None, ["snd"], lambda trs=trs: g.remote_dma_fused(trs, local_sem=T.sem.sent))
+    arrive = sum(len(es) for c0 in T.cores if c0 != core for call in exchange_calls(c0, T, topo) for c, es in call if c == core)
+    part("end")
+    add("G", None, ["sent"], None)
+
+    part("case")
+    add("V", "cs", ["p_c", "c_pat"], lambda: V.tensor_tensor_scan(T.cs[:], T.pat[:], T.pc[:, 0:256], 0.0, op.mult, op.add))
+    case = T.cs[:, 7::8]
+    part("case2")
+    ts("a", ["cs"], T.aa[:, 2:34], case, 0.5 - lift, op.is_gt)
+    ts("a", [], T.aa[:, 36:68], case, 254.5 - lift, op.is_lt)
+    part("case3")
+    tt("colf", ["kdw", "cs"], T.colf[:], case, T.kdw[:], op.add)
+    part("case4")
+    copy("V", "colu", ["colf"], T.colu[:], T.colf[:])
+    part("tabg")
+    copy("V", "tabg", ["colu", "d_tab"], T.tabg[:], T.tabw[:, 0:2048].indirect(T.colu[:, 0:32]))
+    part("l")
+    mm("p_l", ["a", "c_a", "c_w"], T.pl[:, 0:32],
+       [(w, T.aa[:, s + o:s + o + 32]) for o in (0, 34) for w, s in ((T.w1[:], 2), (T.hi[:], 1), (T.bi[:], 1))])
+    part("slot0")
+    add("V", "lf", ["p_l", "c_n16"], lambda: V.tensor_tensor_scan(T.lf[:], T.n16[:], T.pl[:, 0:32], BIG, op.add, op.add))
+    part("slot1")
+    tt("lm", ["lf", "i_park"], T.lm[:], T.lf[:], T.park[:], op.min)
+    part("slot2")
+    copy("V", "su", ["lm"], T.su[:], T.lm[:])
+    part("scat")
+    tt("vw0", ["su", "tabg", "cet", "c_vw"], T.vw[:, 0:768].indirect(T.su[:, 0:16]), T.tabg[:, 0:256], T.cet[:, 0:256], op.add)
+    part("scat1")
+    tt("vw", ["vw0"], T.vw[:, 0:768].indirect(T.su[:, 16:32]), T.tabg[:, 256:512], T.cet[:, 256:512], op.add)
+    part("u0")
+    ts("eu", ["vw"], T.eu[:], T.vw[:, 0:A], 1.0 / 32, op.mult)
+    part("u1")
+    ts("ef", ["eu"], T.ef[:], T.eu[:], -32.0, op.mult)
+    part("u")
+    mm("p_u", ["ef", "i_m16", "c_idf"], T.pc[:, 256:256 + A],
+       [(T.idf[:], T.vw[:, 0:A]), (T.idf[:], T.ef[:]), (T.idf[:], T.m16[:])])
+    part("u2")
+    copy("V", "o2u", ["p_u"], T.o2u[:], T.pc[:, 256:256 + A])
+
+    for c in range(EC):
+        n = "%d" % c
+        pe = T["pe" + n]
+        a0, b0, e0 = 2 * EW * c, 2 * EW * c + EW, EW * c
+        xa, vt = T.xa[:, 16 * e0:16 * (e0 + EW)], T.vt[:, 16 * e0:16 * (e0 + EW)]
+        for h in range(2):
+            part("e%s%s" % ("ab"[h], n))
+            c0 = 256 + a0 + EW * h
+            copy(who(), "g_e" + n, ["o_l", "d_lv"], T.gl[:, 16 * c0:16 * (c0 + EW)], levels(256 + 96 * h + e0, EW))
+        part("e" + n)
+        unwrap("p_e" + n, ["g_e" + n, "c_wd"], pe[:, 0:2 * EW], 256 + a0, 2 * EW)
+        part("x" + n)
+        ts("se" + n, ["p_e" + n], T.se[:, a0:a0 + 2 * EW], pe[:, 0:2 * EW], 0.0, op.is_gt)
+        for h in range(2):
+            mm("p_x" + n, ["se" + n, "abf", "c_idf", "c_w"], pe[:, 256 + EW * h:256 + EW * (h + 1)],
+               [(T.idf[:], T.abf[:, 96 * h + e0:96 * h + e0 + EW]), (T.bi[:], T.se[:, a0:b0]), (T.bi[:], T.se[:, b0:b0 + EW])])
+        part("z" + n)
+        ts("oabu" + n, ["p_x" + n], T.oabu[:, a0:a0 + 2 * EW], pe[:, 256:256 + 2 * EW], float(PAD + NV), op.min, 0.0, op.max)
+        part("xa" + n)
+        copy(who(), "xa" + n, ["oabu" + n, "d_ch", "c_chz"], xa, channels(a0))
+        part("xb" + n)
+        if who() == "V":
+            tt("vt", ["xa" + n], vt, channels(b0), xa, op.add)
+        else:
+            copy("S", "xs", ["oabu" + n, "d_ch", "c_chz"], T.xs[:], channels(b0))
+            part("s")
+            mm("p_s", ["xa" + n, "xs", "c_b"], T.ps[:], [(T.idb[:], xa), (T.idb[:], T.xs[:])])
+            copy("S", "vt", ["p_s"], vt, T.ps[:])
+
+    spans = [(a, b) for a, b in ((0, B * r), (B * r + B, B * N)) if b > a]
+    part("b")
+    for a, b in spans:
+        mm("p_bd", ["snd", "c_b", "arr"], T.pbd[:, a:b],
+           [(T.bc[:], T.sendb[:, 2 * a + 1:2 * b:2]), (T.nbc[:], T.land[:, 2 * a + 1:2 * b:2])])
+    for a, b in spans:
+        mm("p_bs", [], T.pbs[:, a:b], [(T.idb[:], T.sendb[:, 2 * a:2 * b:2]), (T.idb[:], T.land[:, 2 * a:2 * b:2])])
+    part("cb")
+    for a, b in spans:
+        add("S", "cb", ["p_bd"], lambda a=a, b=b: S.activation(T.cb[:, a:b], T.pbd[:, a:b], act.Abs, scale=0.5))
+    part("vb")
+    for a, b in spans:
+        tt("vt", ["cb", "p_bs"], T.vt[:, E + a:E + b], T.pbs[:, a:b], T.cb[:, a:b], op.mult)
+
+    part("out")
+    for i, (m0, n) in enumerate(pieces):
+        for h, q in enumerate(("V", "S")):
+            m = m0 + h * n
+            ww = T.ww[:, 16 * m:16 * (m + n)]
+            copy(q, "w%d_%d" % (h, i), ["vt", "eu"], ww, T.vt[:, 0:Z + 16].indirect(T.eu[:, m:m + n]))
+            copy(q, "y%d" % i, ["w%d_%d" % (h, i), "o2u"], T.yo[:, 16 * m:16 * (m + n)], ww.indirect(T.o2u[:, m:m + n]))
+        dma("Y", "d_y", ["y%d" % i], T.y[:, 16 * m0:16 * (m0 + 2 * n)], T.yo[:, 16 * m0:16 * (m0 + 2 * n)])
+    add("Y", None, ["d_y"], None)
+
+    prog = {}
+    for q in eng:
+        names = CFG[q].split()
+        assert sorted(names) == sorted(parts[q])
+        prog[q] = [x for name in names for x in parts[q][name]]
+    emit(eng, prog, T, {"arr": arrive, "sent": sent})
+
+
+def emit(eng, prog, T, outside):
+    total, left = dict(outside), {}
+    for q in prog:
+        for sig, waits, fn, inc in prog[q]:
+            if sig:
+                total[sig] = total.get(sig, 0) + inc
+                left[sig] = left.get(sig, 0) + 1
+    known = {q: set() for q in prog}
+    carry = {}
+    pos = {q: 0 for q in prog}
+    order, used = [], set()
+    moved = True
+    while moved:
+        moved = False
+        for q in prog:
+            while pos[q] < len(prog[q]):
+                sig, waits, fn, inc = prog[q][pos[q]]
+                if any(left.get(w, 0) for w in waits):
+                    break
+                need = [w for w in waits if w not in known[q]]
+                need = [w for w in need if not any(w in carry.get(v, ()) for v in need if v != w)]
+                for w in need:
+                    known[q].add(w)
+                    known[q] |= carry.get(w, set())
+                used.update(need)
+                if sig:
+                    carry.setdefault(sig, set()).update(known[q])
+                    left[sig] -= 1
+                order.append((q, sig, need, fn, inc))
+                pos[q] += 1
+                moved = True
+    assert all(pos[q] == len(prog[q]) for q in prog)
+    names = {k: k for k in outside}
+    for q, sig, need, fn, inc in order:
+        if sig in used and sig not in names:
+            names[sig] = "s%d" % (len(names) - len(outside))
+    for q, sig, need, fn, inc in order:
+        for w in need:
+            eng[q].wait_ge(T.sem[names[w]], total[w])
+        if fn is not None:
+            ins = fn()
+            if sig in used:
+                ins.then_inc(T.sem[names[sig]], inc)

@@ -1,37 +1,39 @@
-from concourse.bass import DstId, RemoteDMATransfer, IndirectOffsetOnAxis
+from concourse.bass import DstId, RemoteDMATransfer
 from concourse.mybir import AluOpType, ActivationFunctionType
 
 NV, NC, E, B, A, N = 2048, 512, 1536, 64, 112, 8
 Z = E + N * B
 PAD = 16
 BIG = 4096.0
-VDEF = float(32 * Z + 1)
-EC = 3
+EC = 2
 EW = 96 // EC
+XW = 24
+BANKS = (40, 40, 32)
 CFG = {
-    "out": (14, 16, 14, 12),
-    "V": "consts o_cor c1a c0b c0a prm o_l snd_s c1b cey kd cez case kdw case2 case3 cet slot0 abf x0 case4 slot1 tabg "
-         "x1 slot2 z0 scat z1 x2 scat1 z2 u0 u1 xb0 xb1 u2 vb out",
-    "S": "cor bl lv ea ce0 c3a c2b c2a snd_c c3b eb0 ea0 eb1 ea1 ea2 eb2 xa0 xa1 xa2 xb2 cb s out",
-    "P": "c2 c0 c3 c1 l e0 e1 x0 x1 e2 x2 b u s",
-    "Y": "kd1 eb ch kd0 ce1 out",
-    "G": "zer one p wd cf w park tab w2 send idf b m16 end",
+    "out": (12, 20, 8, 20, 24, 28),
+    "V": "consts wds o_cor o_l c000 c010 c011 c001 abf eb0 kd case snd_s act0 act1 cey col se0 cez slot0 slot1 z0 slot2 "
+         "scat vh xb0 colu z1 xb1 xn xa2 sel0 xb2 eu0 vb sel1 y2 eu1 sel2 eu2 y4",
+    "S": "cor ea lv w ce0 c100 c110 c101 c111 ea0 snd_c ea1 eb1 xa0 se1 xa1 tabg xb3 xq xa3 cb s3 y0 y1 y3 y5",
+    "P": "c0 c1 ea0 sw eb0 l x0 d2 ea1 d0 eb1 x1 cw dc2 dc0 d1 dc1 dx0 b s3 dx1 dx2",
+    "Y": "eb bl kd0 ch kd1 ce1 sel tab r y0 y2 y1 y3 y4 y5 out",
+    "G": "zer idb wd sel park swap idh tri tri2 wc b send r end",
 }
 
-F32, BF, I32, U16 = "float32", "bfloat16", "int32", "uint16"
-SCRATCH = {k: ("psum", [128, 512], F32) for k in ("pc", "pe0", "pe1", "pe2", "pl", "pbd", "pbs", "ps")}
+F32, BF, F16, I32, U16 = "float32", "bfloat16", "float16", "int32", "uint16"
+SCRATCH = {k: ("psum", [128, 512], F32) for k in ("pc", "pw", "pe0", "pe1", "pe2", "pbd", "pbs", "ps")}
 for _dt, _bufs in (
-        (BF, dict(lvw=[NV], chw=[NV + 2 * PAD], gl=[7168], zer=[144], one=[128], wd=[144], idb=[128], bc=[128], nbc=[128],
-                  t1=[128], t2=[128], t3=[128], hi=[128], w1=[128], bi=[128], pat=[256], aa=[68], se=[192], xa=[E],
-                  xs=[16 * EW], sendb=[2 * B * N], land=[2 * B * N])),
-        (I32, dict(tabw=[2048], lst=[480], cex=[2, 16, 12], kdx=[32], pi=[4], ti=[4])),
-        (U16, dict(off=[480], prm=[32], colu=[32], su=[32], eu=[A], o2u=[A], oabu=[192])),
-        (F32, dict(abf=[192], cey=[32, 16], cez=[NC], cet=[NC], kdf=[32], kdw=[32], pf=[4], cf=[32], idf=[128], park=[32],
-                   m16=[A], n16=[32], cs=[256], colf=[32], lf=[32], lm=[32], tabg=[NC], vw=[768], ef=[A], vt=[Z + 16],
-                   ww=[16 * A], yo=[16 * A], cb=[B * N]))):
+        (BF, dict(lvw=[NV], chw=[PAD + NV], gk=[8 * NC], ge=[2 * E], zer=[160], wd=[4, 144], idw=[160], bc=[128],
+                  nbc=[128], t1=[128], blk=[128], low=[128], upp=[128], bi=[128], w=[6, 128], sw=[2, 160], pat=[64],
+                  lift=[64], cs=[64], y255=[32], aa=[32], kdb=[32], se=[96], xa=[E], xs=[E], xp=[A], xn=[A], rr=[12 * A],
+                  sendb=[2 * B * N], land=[2 * B * N])),
+        (F16, dict(abf=[192], cey=[32, 16], cez=[NC], vh=[A], sel=[12, 128], wc=[144], idh=[128])),
+        (I32, dict(tabw=[2048], lc=[2, 4, 2, 16], lst=[224], cex=[2, 16, 12], kdx=[32])),
+        (U16, dict(off=[480], colu=[8], su=[32], eu=[A], oabu=[192])),
+        (F32, dict(park=[32], lf=[64], lm=[32], vw=[768], sc=[12 * A], vt=[Z + 16], yo=[16 * A], cb=[B * N]))):
     for _k, _sh in _bufs.items():
         SCRATCH[_k] = ("sbuf", [128] + _sh, _dt)
-SEMAPHORES = ["arr", "sent"] + ["s%d" % i for i in range(100)]
+SCRATCH["seld"] = ("dram", [144, 128], F16)
+SEMAPHORES = ["arr", "sent"] + ["s%d" % i for i in range(110)]
 
 
 def exchange_calls(core, T, topo):
@@ -86,6 +88,9 @@ def rank_program(g, core, T, topo):
     def tt(sig, waits, out, in0, in1, o):
         add("V", sig, waits, lambda: V.tensor_tensor(out, in0, in1, o))
 
+    def scan(sig, waits, out, d0, d1, init, o0, o1):
+        add("V", sig, waits, lambda: V.tensor_tensor_scan(out, d0, d1, init, o0, o1))
+
     def fill(sig, waits, out, c):
         add("V", sig, waits, lambda: V.memset(out, c))
 
@@ -95,20 +100,23 @@ def rank_program(g, core, T, topo):
         else:
             add(q, sig, waits, lambda: S.activation(out, in_, act.Copy))
 
+    def affine(sig, waits, out, in_, scale, bias):
+        if who() == "S":
+            add("S", sig, waits, lambda: S.activation(out, in_, act.Identity, bias=bias, scale=scale))
+        else:
+            ts(sig, waits, out, in_, scale, op.mult, bias, op.add)
+
     def sign(sig, waits, out, in_):
         if who() == "S":
             add("S", sig, waits, lambda: S.activation(out, in_, act.Sign, bias=2.0 ** -120, scale=2.0 ** 16))
         else:
             ts(sig, waits, out, in_, 0.0, op.is_lt, -2.0, op.mult)
 
-    def mm(sig, waits, out, pairs):
-        for i, (lhs, rhs) in enumerate(pairs):
-            last = i == len(pairs) - 1
+    def mm(sig, waits, terms, start=True, stop=True):
+        for i, (out, lhs, rhs) in enumerate(terms):
+            last = i == len(terms) - 1
             add("P", sig if last else None, waits if i == 0 else [],
-                lambda lhs=lhs, rhs=rhs, i=i, last=last: P.matmul(out, lhs, rhs, i == 0, last))
-
-    def unwrap(sig, waits, out, c0, n):
-        mm(sig, waits, out, [(T.wd[:, 15 - t:143 - t], T.gl[:, 16 * c0 + t:16 * (c0 + n):16]) for t in range(16)])
+                lambda out=out, lhs=lhs, rhs=rhs, a=start and i == 0, b=stop and last: P.matmul(out, lhs, rhs, a, b))
 
     def iota(sig, out, pattern, base, cm):
         add("G", sig, [], lambda: g.iota(out, pattern, base, cm, allow_small_or_imprecise_dtypes=True))
@@ -120,109 +128,109 @@ def rank_program(g, core, T, topo):
         return T.lvw[:, 0:NV].indirect(T.off[:, c0:c0 + n])
 
     def channels(c0):
-        return T.chw[:, 0:NV + 2 * PAD].indirect(T.oabu[:, c0:c0 + EW])
+        return T.chw[:, 0:PAD + NV].indirect(T.oabu[:, c0:c0 + XW])
 
-    lift = sum(8.5 * 2 ** kp for kp in range(4) if "c%da" % kp in on_s)
-
-    load("cor", "d_cor", [], T.lst[:, 0:256], T.cor[:])
-    load("bl", "d_bl", [], T.lst[:, 448:480], T.bl[:])
+    load("cor", "d_cor", [], T.lc[:], T.cor[:])
+    load("bl", "d_bl", [], T.lst[:, 192:224], T.bl[:])
     load("kd0", "d_kd", [], T.kdx[:, 0:16], T.kd[0::2, :])
     load("kd1", "d_kd", [], T.kdx[:, 16:32], T.kd[1::2, :])
     load("lv", "d_lv", ["lvz"], T.lvw[0::16, :], T.lv[:])
-    load("ea", "d_l", ["lvz"], T.lst[:, 256:352], T.ea[:])
-    load("eb", "d_l", ["lvz"], T.lst[:, 352:448], T.eb[:])
+    load("ea", "d_l", [], T.lst[:, 0:96], T.ea[:])
+    load("eb", "d_l", [], T.lst[:, 96:192], T.eb[:])
     load("ce0", "d_ce", [], T.cex[:, 0], T.ce[0::2, :])
     load("ce1", "d_ce", [], T.cex[:, 1], T.ce[1::2, :])
-    load("ch", "d_ch", [], T.chw[:, PAD:PAD + NV], T.ch[:])
-    part("tab")
-    add("G", "d_tab", ["c_t"], lambda: g.indirect_dma_start(
-        T.tabw[:], None, T.tab[:], IndirectOffsetOnAxis(ap=T.ti[:, 0:1], axis=0), bounds_check=15), 16)
+    load("ch", "d_ch", ["lvz"], T.chw[:, PAD:PAD + NV], T.ch[:])
+    for k in range(8):
+        load("tab", "d_tab", [], T.tabw[16 * k:16 * k + 16, :], T.tab[:])
 
     diag, blocks = [[1, 128]], [[16, 8], [0, 16]]
-    part("p")
-    add("G", "i_p", [], lambda: g.iota(T.pi[:, 0:1], [[0, 1]], 0, 1))
+    zer = T.zer[:, 0:128]
     part("zer")
-    iota("zer", T.zer[:], [[0, 144]], 0, 0)
-    part("one")
-    iota("one", T.one[:], [[0, 128]], 1, 0)
-    part("cf")
-    iota("i_cf", T.cf[:], [[1, 32]], 0, 0)
+    idb = T.idw[:, 16:144]
+    iota("zer", T.zer[:], [[0, 160]], 0, 0)
+    part("idb")
+    pick("c_id", ["zer"], T.idw[:], T.zer[:], [[1, 160]], op.not_equal, 1.0, -16, -1)
+    part("idh")
+    pick("c_idh", ["zer"], T.idh[:], zer, diag, op.not_equal, 1.0, 0, -1)
     part("park")
     iota("i_park", T.park[:], [[16, 32]], A, 1)
     part("wd")
-    pick("c_wd", ["zer"], T.wd[:], T.zer[:], [[16, 9], [-200, 16]], op.not_equal, -0.5, 3000, -1)
-    part("w")
-    pick("t1", ["one"], T.t1[:], T.one[:], diag, op.is_gt, 0.0, 0, -1)
-    pick("t2", [], T.t2[:], T.one[:], [[-1, 128]], op.is_ge, 0.0, 0, 1)
-    pick("t3", ["t1"], T.t3[:], T.t1[:], [[-16, 8], [0, 16]], op.is_ge, 0.0, 0, 1)
-    part("w2")
-    pick("c_w", ["t2"], T.hi[:], T.t2[:], blocks, op.is_ge, 0.0, 15, -1)
-    pick("c_w", ["t3"], T.w1[:], T.t3[:], diag, op.not_equal, -BIG, 0, -1)
-    pick("c_w", ["zer"], T.bi[:], T.zer[:, 0:128], diag, op.not_equal, BIG, 0, -1)
-    part("idf")
-    pick("c_idf", ["zer"], T.idf[:], T.zer[:, 0:128], diag, op.not_equal, 1.0, 0, -1)
+    pick("c_wd0", ["zer"], T.wd[:, 0], T.zer[:, 0:144], [[16, 9], [-200, 16]], op.not_equal, -0.5, 3000, -1)
+    part("wc")
+    pick("c_wc", ["zer"], T.wc[:], T.zer[:, 0:144], [[16, 9], [-200, 16]], op.not_equal, 1.0, 3012, -1)
+    part("tri")
+    pick("t1", ["zer"], T.t1[:], zer, [[-16, 8], [0, 16]], op.is_gt, 1.0, -15, 1)
+    pick("c_tri", [], T.bi[:], zer, diag, op.not_equal, BIG, 0, -1)
+    pick("blk", ["t1"], T.blk[:], T.t1[:], [[-16, 8], [0, 16]], op.is_ge, 0.0, 0, 1)
+    part("tri2")
+    pick("c_tri", ["blk"], T.low[:], T.blk[:], diag, op.is_gt, 0.0, 0, -1)
+    pick("c_tri", [], T.upp[:], T.blk[:], [[-1, 128]], op.is_gt, 0.0, 0, 1)
+    part("swap")
+    pick("c_sw", ["c_id"], T.sw[:, 0], T.idw[:], [[0, 5], [1, 2], [0, 16]], op.is_gt, 0.0, 0, 0)
+    pick("c_sw", [], T.sw[:, 1], T.idw[:], [[0, 5], [-1, 2], [0, 16]], op.is_gt, 0.0, 1, 0)
     part("b")
-    pick("c_b", ["zer"], T.idb[:], T.zer[:, 0:128], diag, op.not_equal, 1.0, 0, -1)
-    pick("c_b", [], T.bc[:], T.zer[:, 0:128], blocks, op.not_equal, 1.0, 0, -1)
-    pick("c_b", [], T.nbc[:], T.zer[:, 0:128], blocks, op.not_equal, -1.0, 0, -1)
-    part("m16")
-    pieces, m0 = [], 0
-    for n in CFG["out"]:
-        iota("i_m16", T.m16[:, m0:m0 + 2 * n], [[0, 2], [16, n]], 0, 0)
-        pieces.append((m0, n))
-        m0 += 2 * n
+    pick("c_b", ["zer"], T.bc[:], zer, blocks, op.not_equal, 1.0, 0, -1)
+    pick("c_b", [], T.nbc[:], zer, blocks, op.not_equal, -1.0, 0, -1)
+    part("sel")
+    pick("c_sel0", ["zer"], T.sel[:, 0], zer, blocks, op.not_equal, 1.0, 0, -1)
+    dma("Y", "d_sel0", ["c_sel0"], T.seld[16:144, :], T.sel[:, 0])
+    dma("Y", "d_sel0", [], T.seld[1:16, :], T.sel[1:16, 0])
+    for a in range(1, 12):
+        dma("Y", "d_sel", ["d_sel0"], T.sel[:, a], T.seld[16 - a:144 - a, :])
+    part("r")
+    w0 = 12 * BANKS[0]
+    iota("i_r", T.rr[:, 0:w0], [[0, BANKS[0]], [-8192, 12]], 5 * 8192, 0)
+    pick("c_r0", ["i_r"], T.rr[:, 0:w0:12], T.rr[:, 0:w0:12], [[0, BANKS[0]]], op.is_gt, 2.0 ** 21, 0, 0)
+    for b in (1, 2):
+        dma("Y", "d_r", ["c_r0"], T.rr[:, b * w0:b * w0 + 12 * BANKS[b]], T.rr[:, 0:12 * BANKS[b]])
+    part("w")
+    for k in range(6):
+        affine("c_w", ["c_id"], T.w[:, k], idb, -BIG * (2 * k + 1), 0.0)
+    part("wds")
+    for kp in range(1, 4):
+        affine("c_wd", ["c_wd0"], T.wd[:, kp], T.wd[:, 0], 2.0 ** kp, 0.0)
 
+    lift = sum(0.5 * 2 ** (4 * kk + kp) for kk in range(2) for kp in range(4) if "c%d0%d" % (kk, kp // 2) in on_s)
     part("consts")
     fill("lvz", [], T.lvw[:], 0.0)
-    ts("c_t", ["i_p"], T.ti[:, 0:1], T.pi[:, 0:1], 15, op.bitwise_and)
-    fill("pat2", [], T.pat[:], 2.0)
-    ts("c_t32", ["c_t"], T.pf[:, 0:1], T.ti[:, 0:1], 32.0, op.mult)
-    fill("c_pat", ["pat2"], T.pat[:, 0::8], 0.0)
-    fill("c_cey", [], T.cey[:, :, 0:1], VDEF)
-    fill("c_cey", [], T.cey[:, :, 13:16], VDEF)
+    fill("c_pat", [], T.pat[:, 0::2], 0.0)
+    fill("c_pat", [], T.pat[:, 1::2], 16.0)
+    fill("c_lift", [], T.lift[:, 0::2], 0.0)
+    fill("c_lift", [], T.lift[:, 1::2], lift)
     fill("c_chz", [], T.chw[:, 0:PAD], 0.0)
-    fill("c_chz", [], T.chw[:, PAD + NV:], 0.0)
     fill("vt", [], T.vt[:, Z:Z + 16], 0.0)
     fill("vt", [], T.vt[:, E + B * r:E + B * r + B], 0.0)
-    fill("c_vw", [], T.vw[:, 0:A], VDEF)
-    fill("c_a", [], T.aa[:, 1::34], 0.5)
-    fill("c_n16", [], T.n16[:], -16.0)
+    fill("c_vw", [], T.vw[:, 0:A], float(Z))
+    copy("V", "c_cey", ["zer"], T.cey[:, :, 12:16], zer)
     part("o_cor")
-    copy("V", "o_cor", ["d_cor"], T.off[:, 0:256:2], T.lst[:, 128:256])
-    copy("V", "o_cor", [], T.off[:, 1:256:2], T.lst[:, 0:128])
-    copy("V", "o_bl", ["d_bl"], T.off[:, 448:480], T.lst[:, 448:480])
-    part("o_l")
-    copy("V", "o_l", ["d_l"], T.off[:, 256:448], T.lst[:, 256:448])
-    part("abf")
-    ts("abf", ["d_l"], T.abf[:], T.lst[:, 256:448], PAD - BIG, op.add)
-    part("kd")
-    ts("kdf", ["d_kd"], T.kdf[:], T.kdx[:], 256.0, op.mult, lift, op.add)
-    part("prm")
-    ts("c_prm", ["c_t32", "i_cf"], T.prm[:], T.cf[:], T.pf[:, 0:1], op.add)
-
-    part("cey")
-    for k in range(2):
-        ts("cey", ["d_ce"], T.cey[:, k::2, 1:13], T.cex[:, k], 32.0, op.mult, 1.0, op.add)
-    part("kdw")
-    add("V", "kdw", ["kdf"], lambda: V.transpose(T.kdw[:], T.kdf[:]))
-    part("cez")
-    add("V", "cez", ["cey", "c_cey"], lambda: V.transpose(T.cez[:], T.cey[:]))
-    part("cet")
-    copy(who(), "cet", ["cez", "c_prm"], T.cet[:], T.cez[:, 0:NC].indirect(T.prm[:, 0:32]))
-
-    for kp in range(4):
+    for kk in range(2):
         for h in range(2):
-            part("c%d%s" % (kp, "ab"[h]))
-            assert (who() == "S") == ("c%da" % kp in on_s)
-            c0 = 64 * kp + 32 * h
-            sign("g_c%d" % kp, ["d_lv", "o_cor"], T.gl[:, 16 * c0:16 * (c0 + 32)], levels(c0, 32))
-        part("c%d" % kp)
-        unwrap("p_c", ["g_c%d" % kp, "c_wd"], T.pc[:, 3 - kp:256:4], 64 * kp, 64)
+            copy("V", "o_cor%d" % kk, ["d_cor"], T.off[:, 128 * kk + 64 * h:128 * kk + 64 * h + 64], T.lc[:, kk, :, h, :])
+    part("o_l")
+    copy("V", "o_l", ["d_l", "d_bl"], T.off[:, 256:480], T.lst[:])
+    part("abf")
+    ts("abf", ["d_l"], T.abf[:], T.lst[:, 0:192], -1024.0, op.add)
+    part("kd")
+    ts("kdb", ["d_kd"], T.kdb[:], T.kdx[:], 256.0, op.mult)
+
+    for j in range(2):
+        for kk in range(2):
+            for h in range(2):
+                part("c%d%d%d" % (kk, h, j))
+                assert (who() == "S") == ("c%d0%d" % (kk, j) in on_s)
+                p0 = 2048 * j + 2 * h + 1 - kk
+                sign("g_c%d" % j, ["d_lv", "o_cor%d" % kk], T.gk[:, p0:2048 * (j + 1):4], levels(128 * kk + 64 * h + 32 * j, 32))
+        part("c%d" % j)
+        terms = [(T.pc[:, 0:64], T.wd[:, kp, 15 - t:143 - t], T.gk[:, 1024 * kp + 64 * t:1024 * kp + 64 * t + 64])
+                 for kp in (2 * j, 2 * j + 1) for t in range(16)]
+        if j == 0:
+            mm(None, ["c_id", "c_lift"], [(T.pc[:, 0:64], idb, T.lift[:])], stop=False)
+        mm("p_c" if j else None, ["g_c%d" % j, "c_wd0", "c_wd"], terms, start=False, stop=j == 1)
 
     part("snd_s")
-    sign("snd", ["o_bl", "d_lv"], T.sendb[:, 1::2], levels(448, 32))
+    sign("snd", ["o_l", "d_lv"], T.sendb[:, 1::2], levels(448, 32))
     part("snd_c")
-    copy(who(), "snd", ["o_bl", "d_ch"], T.sendb[:, 0::2], T.chw[:, PAD:PAD + NV].indirect(T.off[:, 448:480]))
+    copy(who(), "snd", ["o_l", "d_ch"], T.sendb[:, 0::2], T.chw[:, PAD:PAD + NV].indirect(T.off[:, 448:480]))
     part("send")
     sent = 0
     for call in exchange_calls(core, T, topo):
@@ -240,76 +248,128 @@ def rank_program(g, core, T, topo):
     add("G", None, ["sent"], None)
 
     part("case")
-    add("V", "cs", ["p_c", "c_pat"], lambda: V.tensor_tensor_scan(T.cs[:], T.pat[:], T.pc[:, 0:256], 0.0, op.mult, op.add))
-    case = T.cs[:, 7::8]
-    part("case2")
-    ts("a", ["cs"], T.aa[:, 2:34], case, 0.5 - lift, op.is_gt)
-    ts("a", [], T.aa[:, 36:68], case, 254.5 - lift, op.is_lt)
-    part("case3")
-    tt("colf", ["kdw", "cs"], T.colf[:], case, T.kdw[:], op.add)
-    part("case4")
-    copy("V", "colu", ["colf"], T.colu[:], T.colf[:])
-    part("tabg")
-    copy("V", "tabg", ["colu", "d_tab"], T.tabg[:], T.tabw[:, 0:2048].indirect(T.colu[:, 0:32]))
+    scan("cs", ["p_c", "c_pat"], T.cs[:], T.pat[:], T.pc[:, 0:64], 0.0, op.mult, op.add)
+    case = T.cs[:, 1::2]
+    part("act0")
+    ts("y255", ["cs"], T.y255[:], case, 0.5, op.is_gt, 255.0, op.mult)
+    part("act1")
+    tt("a", ["y255"], T.aa[:], case, T.y255[:], op.not_equal)
     part("l")
-    mm("p_l", ["a", "c_a", "c_w"], T.pl[:, 0:32],
-       [(w, T.aa[:, s + o:s + o + 32]) for o in (0, 34) for w, s in ((T.w1[:], 2), (T.hi[:], 1), (T.bi[:], 1))])
+    a0, a1, pl = T.aa[:, 0::2], T.aa[:, 1::2], 128
+    mm("p_l", ["a", "c_tri", "c_w", "c_id"], [(T.pc[:, pl:pl + 16], T.low[:], a0)])
+    mm("p_l", [], [(T.pc[:, pl + 32:pl + 48], T.upp[:], a0), (T.pc[:, pl + 32:pl + 33], T.bi[:], T.aa[:, 30:31]),
+                   (T.pc[:, pl + 32:pl + 48], T.low[:], a1)])
+    for h in range(2):
+        o = pl + 16 + 32 * h
+        mm("p_l", [], [(T.pc[:, o:o + 16], idb, T.aa[:, h::2]), (T.pc[:, o + 1:o + 16], T.bi[:], T.aa[:, h:30:2]),
+                       (T.pc[:, o:o + 16], T.w[:, 0], T.aa[:, h::2])])
     part("slot0")
-    add("V", "lf", ["p_l", "c_n16"], lambda: V.tensor_tensor_scan(T.lf[:], T.n16[:], T.pl[:, 0:32], BIG, op.add, op.add))
+    scan("lf", ["p_l", "zer"], T.lf[:], T.zer[:, 0:64], T.pc[:, pl:pl + 64], BIG - 1, op.add, op.add)
     part("slot1")
-    tt("lm", ["lf", "i_park"], T.lm[:], T.lf[:], T.park[:], op.min)
+    for h in range(2):
+        tt("lm", ["lf", "i_park"], T.lm[:, h::2], T.lf[:, 16 + 32 * h:32 + 32 * h], T.park[:, h::2], op.min)
     part("slot2")
     copy("V", "su", ["lm"], T.su[:], T.lm[:])
+
+    part("cey")
+    for k in range(2):
+        copy("V", "cey", ["d_ce"], T.cey[:, k::2, 0:12], T.cex[:, k])
+    part("sw")
+    for k in range(2):
+        out = T.pw[:, k:32:2]
+        mm("p_sw", ["cs", "kdb", "c_sw", "c_id"],
+           [(out, idb, T.kdb[:, 16 * k:16 * k + 16])]
+           + [(out, T.sw[:, k, 16 * (1 + k - h):16 * (1 + k - h) + 128], T.cs[:, 1 + 2 * h::4]) for h in range(2)])
+    part("col")
+    copy("V", "cey", ["p_sw", "c_cey"], T.cey[:, :, 12], T.pw[:, 0:32])
+    part("cez")
+    add("V", "cez", ["cey"], lambda: V.transpose(T.cez[:], T.cey[:]))
     part("scat")
-    tt("vw0", ["su", "tabg", "cet", "c_vw"], T.vw[:, 0:768].indirect(T.su[:, 0:16]), T.tabg[:, 0:256], T.cet[:, 0:256], op.add)
-    part("scat1")
-    tt("vw", ["vw0"], T.vw[:, 0:768].indirect(T.su[:, 16:32]), T.tabg[:, 256:512], T.cet[:, 256:512], op.add)
-    part("u0")
-    ts("eu", ["vw"], T.eu[:], T.vw[:, 0:A], 1.0 / 32, op.mult)
-    part("u1")
-    ts("ef", ["eu"], T.ef[:], T.eu[:], -32.0, op.mult)
-    part("u")
-    mm("p_u", ["ef", "i_m16", "c_idf"], T.pc[:, 256:256 + A],
-       [(T.idf[:], T.vw[:, 0:A]), (T.idf[:], T.ef[:]), (T.idf[:], T.m16[:])])
-    part("u2")
-    copy("V", "o2u", ["p_u"], T.o2u[:], T.pc[:, 256:256 + A])
+    copy("V", "vw", ["su", "cez", "c_vw"], T.vw[:, 0:768].indirect(T.su[:, 0:32]), T.cez[:])
+    part("vh")
+    copy("V", "vh", ["vw"], T.vh[:], T.vw[:, 0:A])
+    part("cw")
+    mm("p_cw", ["vh", "c_wc"], [(T.pw[:, 64:71], T.wc[:, 15 - t:143 - t], T.vh[:, t::16]) for t in range(16)])
+    part("colu")
+    ts("colu", ["p_cw"], T.colu[:, 0:7], T.pw[:, 64:71], 2047.0, op.min)
+    part("tabg")
+    affine("xp", ["colu", "d_tab"], T.xp[:], T.tabw[:, 0:2048].indirect(T.colu[:, 0:7]), 1.0, -5.5)
+    part("xn")
+    affine("xn", ["xp"], T.xn[:], T.xp[:], -1.0, 0.0)
+    part("xq")
+    add("S", "xq", ["xp", "d_r"], lambda: S.activation(T.rr[:, 11::12], T.xp[:], act.Square, scale=64.0))
+
+    m0 = 0
+    for b, n in enumerate(BANKS):
+        pd, sl = T["pe%d" % b], slice(m0, m0 + n)
+        order = [(j, (j + 1) % 12) for j in range(12)]
+        part("d%d" % b)
+        mm(None, ["zer", "d_lv"] + ["oabu%d" % c for c in range(EC) if c == b],
+           [(pd[:, 0:12 * n], zer, T.lvw[:, 0:12 * n])], stop=False)
+        part("dc%d" % b)
+        mm(None, ["vh", "d_sel"], [(pd[:, j:12 * n:12], T.sel[:, a], T.vh[:, sl]) for j, a in order], start=False, stop=False)
+        part("dx%d" % b)
+        for j, a in sorted(order, key=lambda ja: -ja[1]):
+            x = "xp" if a > 5 else "xn"
+            mm("p_d%d" % b, [x], [(pd[:, j:12 * n:12], T.w[:, abs(2 * a - 11) // 2], T[x][:, sl])], start=False, stop=False)
+        mm("p_d%d" % b, ["xq"], [(pd[:, 11:12 * n:12], idb, T.rr[:, 12 * m0 + 11:12 * (m0 + n):12])], start=False)
+        part("sel%d" % b)
+        scan("sc%d" % b, ["p_d%d" % b], T.sc[:, 12 * m0:12 * (m0 + n)], T.rr[:, 12 * m0:12 * (m0 + n)], pd[:, 0:12 * n],
+             0.0, op.add, op.min)
+        part("eu%d" % b)
+        ts("eu%d" % b, ["sc%d" % b], T.eu[:, sl], T.sc[:, 12 * m0 + 11:12 * (m0 + n):12], 121 * 1024.0, op.add, float(Z), op.min)
+        m0 += n
 
     for c in range(EC):
         n = "%d" % c
         pe = T["pe" + n]
         a0, b0, e0 = 2 * EW * c, 2 * EW * c + EW, EW * c
-        xa, vt = T.xa[:, 16 * e0:16 * (e0 + EW)], T.vt[:, 16 * e0:16 * (e0 + EW)]
+        low = 0.0
         for h in range(2):
             part("e%s%s" % ("ab"[h], n))
-            c0 = 256 + a0 + EW * h
-            copy(who(), "g_e" + n, ["o_l", "d_lv"], T.gl[:, 16 * c0:16 * (c0 + EW)], levels(256 + 96 * h + e0, EW))
-        part("e" + n)
-        unwrap("p_e" + n, ["g_e" + n, "c_wd"], pe[:, 0:2 * EW], 256 + a0, 2 * EW)
+            low += 0.5 * (who() == "S")
+            c0 = a0 + EW * h
+            sign("g_" + here[0], ["o_l", "d_lv"], T.ge[:, 16 * c0:16 * (c0 + EW)], levels(256 + 96 * h + e0, EW))
+            mm("p_e" + n if h else None, ["g_" + here[0], "c_wd0"],
+               [(pe[:, 0:EW], T.wd[:, 0, 15 - t:143 - t], T.ge[:, 16 * c0 + t:16 * (c0 + EW):16]) for t in range(16)],
+               start=h == 0, stop=h == 1)
+        part("se" + n)
+        se = T.se[:, e0:e0 + EW]
+        if who() == "S":
+            add("S", "se" + n, ["p_e" + n], lambda se=se, pe=pe, low=low: S.activation(se, pe[:, 0:EW], act.Abs, bias=low - 1.0))
+        else:
+            ts("se" + n, ["p_e" + n], se, pe[:, 0:EW], 1.0 - low, op.not_equal)
         part("x" + n)
-        ts("se" + n, ["p_e" + n], T.se[:, a0:a0 + 2 * EW], pe[:, 0:2 * EW], 0.0, op.is_gt)
         for h in range(2):
-            mm("p_x" + n, ["se" + n, "abf", "c_idf", "c_w"], pe[:, 256 + EW * h:256 + EW * (h + 1)],
-               [(T.idf[:], T.abf[:, 96 * h + e0:96 * h + e0 + EW]), (T.bi[:], T.se[:, a0:b0]), (T.bi[:], T.se[:, b0:b0 + EW])])
+            out = pe[:, 256 + EW * h:256 + EW * (h + 1)]
+            mm("p_x" + n, ["se" + n, "abf", "c_idh", "c_w"],
+               [(out, T.idh[:], T.abf[:, 96 * h + e0:96 * h + e0 + EW]), (out, T.w[:, 0], se)])
         part("z" + n)
-        ts("oabu" + n, ["p_x" + n], T.oabu[:, a0:a0 + 2 * EW], pe[:, 256:256 + 2 * EW], float(PAD + NV), op.min, 0.0, op.max)
+        ts("oabu" + n, ["p_x" + n], T.oabu[:, a0:a0 + 2 * EW], pe[:, 256:256 + 2 * EW], 1024.0 + PAD, op.add)
+    done = ["vt"]
+    for i in range(96 // XW):
+        n, c, e0 = "%d" % i, XW * i // EW, XW * i
+        a0, cols = e0 + EW * c, slice(16 * e0, 16 * (e0 + XW))
         part("xa" + n)
-        copy(who(), "xa" + n, ["oabu" + n, "d_ch", "c_chz"], xa, channels(a0))
+        copy(who(), "xa" + n, ["oabu%d" % c, "d_ch", "c_chz"], T.xa[:, cols], channels(a0))
         part("xb" + n)
         if who() == "V":
-            tt("vt", ["xa" + n], vt, channels(b0), xa, op.add)
+            tt("vt", ["xa" + n], T.vt[:, cols], channels(a0 + EW), T.xa[:, cols], op.add)
         else:
-            copy("S", "xs", ["oabu" + n, "d_ch", "c_chz"], T.xs[:], channels(b0))
-            part("s")
-            mm("p_s", ["xa" + n, "xs", "c_b"], T.ps[:], [(T.idb[:], xa), (T.idb[:], T.xs[:])])
-            copy("S", "vt", ["p_s"], vt, T.ps[:])
+            copy("S", "xs" + n, ["oabu%d" % c, "d_ch", "c_chz"], T.xs[:, cols], channels(a0 + EW))
+            part("s" + n)
+            out = T.ps[:, 0:16 * XW]
+            mm("p_s" + n, ["xa" + n, "xs" + n, "c_id"] + done[1:], [(out, idb, T.xa[:, cols]), (out, idb, T.xs[:, cols])])
+            copy("S", "vt" + n, ["p_s" + n], T.vt[:, cols], out)
+            done.append("vt" + n)
 
     spans = [(a, b) for a, b in ((0, B * r), (B * r + B, B * N)) if b > a]
     part("b")
     for a, b in spans:
-        mm("p_bd", ["snd", "c_b", "arr"], T.pbd[:, a:b],
-           [(T.bc[:], T.sendb[:, 2 * a + 1:2 * b:2]), (T.nbc[:], T.land[:, 2 * a + 1:2 * b:2])])
+        mm("p_bd", ["snd", "c_b", "arr"], [(T.pbd[:, a:b], T.bc[:], T.sendb[:, 2 * a + 1:2 * b:2]),
+                                           (T.pbd[:, a:b], T.nbc[:], T.land[:, 2 * a + 1:2 * b:2])])
     for a, b in spans:
-        mm("p_bs", [], T.pbs[:, a:b], [(T.idb[:], T.sendb[:, 2 * a:2 * b:2]), (T.idb[:], T.land[:, 2 * a:2 * b:2])])
+        mm("p_bs", ["c_id"], [(T.pbs[:, a:b], idb, T.sendb[:, 2 * a:2 * b:2]), (T.pbs[:, a:b], idb, T.land[:, 2 * a:2 * b:2])])
     part("cb")
     for a, b in spans:
         add("S", "cb", ["p_bd"], lambda a=a, b=b: S.activation(T.cb[:, a:b], T.pbd[:, a:b], act.Abs, scale=0.5))
@@ -317,25 +377,26 @@ def rank_program(g, core, T, topo):
     for a, b in spans:
         tt("vt", ["cb", "p_bs"], T.vt[:, E + a:E + b], T.pbs[:, a:b], T.cb[:, a:b], op.mult)
 
+    m0 = 0
+    for i, n in enumerate(CFG["out"]):
+        need = ["eu%d" % b for b in range(3) if sum(BANKS[:b]) < m0 + n and m0 < sum(BANKS[:b + 1])]
+        yo = T.yo[:, 16 * m0:16 * (m0 + n)]
+        part("y%d" % i)
+        copy(who(), "y%d" % i, done + need, yo, T.vt[:, 0:Z + 16].indirect(T.eu[:, m0:m0 + n]))
+        dma("Y", "d_y", ["y%d" % i], T.y[:, 16 * m0:16 * (m0 + n)], yo)
+        m0 += n
     part("out")
-    for i, (m0, n) in enumerate(pieces):
-        for h, q in enumerate(("V", "S")):
-            m = m0 + h * n
-            ww = T.ww[:, 16 * m:16 * (m + n)]
-            copy(q, "w%d_%d" % (h, i), ["vt", "eu"], ww, T.vt[:, 0:Z + 16].indirect(T.eu[:, m:m + n]))
-            copy(q, "y%d" % i, ["w%d_%d" % (h, i), "o2u"], T.yo[:, 16 * m:16 * (m + n)], ww.indirect(T.o2u[:, m:m + n]))
-        dma("Y", "d_y", ["y%d" % i], T.y[:, 16 * m0:16 * (m0 + 2 * n)], T.yo[:, 16 * m0:16 * (m0 + 2 * n)])
     add("Y", None, ["d_y"], None)
 
+    emit(eng, parts, T, {"arr": arrive, "sent": sent})
+
+
+def emit(eng, parts, T, outside):
     prog = {}
     for q in eng:
         names = CFG[q].split()
-        assert sorted(names) == sorted(parts[q])
+        assert sorted(names) == sorted(parts[q]), (q, set(names) ^ set(parts[q]))
         prog[q] = [x for name in names for x in parts[q][name]]
-    emit(eng, prog, T, {"arr": arrive, "sent": sent})
-
-
-def emit(eng, prog, T, outside):
     total, left = dict(outside), {}
     for q in prog:
         for sig, waits, fn, inc in prog[q]:
@@ -366,7 +427,7 @@ def emit(eng, prog, T, outside):
                 order.append((q, sig, need, fn, inc))
                 pos[q] += 1
                 moved = True
-    assert all(pos[q] == len(prog[q]) for q in prog)
+    assert all(pos[q] == len(prog[q]) for q in prog), [(q, prog[q][pos[q]][:2]) for q in prog if pos[q] < len(prog[q])]
     names = {k: k for k in outside}
     for q, sig, need, fn, inc in order:
         if sig in used and sig not in names:

from concourse.bass import DstId, RemoteDMATransfer
from concourse.mybir import AluOpType, ActivationFunctionType

NV, NC, E, B, A, N = 2048, 512, 1536, 64, 112, 8
Z = E + N * B
PAD = 16
BIG = 4096.0
EC = 2
EW = 96 // EC
XW = 24
BANKS = (40, 40, 32)
CFG = {
    "out": (12, 20, 8, 20, 24, 28),
    "V": "consts wds o_cor o_l c000 c010 c011 c001 abf eb0 kd case snd_s act0 act1 cey col se0 cez slot0 slot1 z0 slot2 "
         "scat vh xb0 colu z1 xb1 xn xa2 sel0 xb2 eu0 vb sel1 y2 eu1 sel2 eu2 y4",
    "S": "cor ea lv w ce0 c100 c110 c101 c111 ea0 snd_c ea1 eb1 xa0 se1 xa1 tabg xb3 xq xa3 cb s3 y0 y1 y3 y5",
    "P": "c0 c1 ea0 sw eb0 l x0 d2 ea1 d0 eb1 x1 cw dc2 dc0 d1 dc1 dx0 b s3 dx1 dx2",
    "Y": "eb bl kd0 ch kd1 ce1 sel tab r y0 y2 y1 y3 y4 y5 out",
    "G": "zer idb wd sel park swap idh tri tri2 wc b send r end",
}

F32, BF, F16, I32, U16 = "float32", "bfloat16", "float16", "int32", "uint16"
SCRATCH = {k: ("psum", [128, 512], F32) for k in ("pc", "pw", "pe0", "pe1", "pe2", "pbd", "pbs", "ps")}
for _dt, _bufs in (
        (BF, dict(lvw=[NV], chw=[PAD + NV], gk=[8 * NC], ge=[2 * E], zer=[160], wd=[4, 144], idw=[160], bc=[128],
                  nbc=[128], t1=[128], blk=[128], low=[128], upp=[128], bi=[128], w=[6, 128], sw=[2, 160], pat=[64],
                  lift=[64], cs=[64], y255=[32], aa=[32], kdb=[32], se=[96], xa=[E], xs=[E], xp=[A], xn=[A], rr=[12 * A],
                  sendb=[2 * B * N], land=[2 * B * N])),
        (F16, dict(abf=[192], cey=[32, 16], cez=[NC], vh=[A], sel=[12, 128], wc=[144], idh=[128])),
        (I32, dict(tabw=[2048], lc=[2, 4, 2, 16], lst=[224], cex=[2, 16, 12], kdx=[32])),
        (U16, dict(off=[480], colu=[8], su=[32], eu=[A], oabu=[192])),
        (F32, dict(park=[32], lf=[64], lm=[32], vw=[768], sc=[12 * A], vt=[Z + 16], yo=[16 * A], cb=[B * N]))):
    for _k, _sh in _bufs.items():
        SCRATCH[_k] = ("sbuf", [128] + _sh, _dt)
SCRATCH["seld"] = ("dram", [144, 128], F16)
SEMAPHORES = ["arr", "sent"] + ["s%d" % i for i in range(110)]


def exchange_calls(core, T, topo):
    near = [c for c in T.cores if c != core and c in topo.cores_of(core)]
    far = [c for c in T.cores if c != core and c not in near]
    me = T.rank_of(core)
    far.sort(key=lambda c: (T.rank_of(c) - me) % N)
    out = topo.engines(core, far[0])
    first, second = far[:len(out) // 2], far[len(out) // 2:]
    call1 = [(c, out[2 * i:2 * i + 2]) for i, c in enumerate(first)]
    w = len(out) // len(second)
    call2 = [(c, out[w * i:w * i + w]) for i, c in enumerate(second)]
    for c in near:
        call1.append((c, [e for e in topo.engines(core, c) if e not in out][0:4:2]))
    return [call1, call2]


def rank_program(g, core, T, topo):
    r = T.rank_of(core)
    if r is None:
        return
    op = AluOpType
    act = ActivationFunctionType
    V, S, P = g.vector, g.scalar, g.tensor
    eng = {"V": V, "S": S, "P": P, "Y": g.sync, "G": g}
    parts = {q: {} for q in eng}
    here = [""]
    on_s = CFG["S"].split()

    def part(name):
        here[0] = name

    def who():
        return "S" if here[0] in on_s else "V"

    def add(q, sig, waits, fn, inc=1):
        parts[q].setdefault(here[0], []).append((sig, list(waits), fn, inc))

    def dma(q, sig, waits, out, in_):
        add(q, sig, waits, lambda: eng[q].dma_start(out, in_), 16)

    def load(name, sig, waits, out, in_):
        part(name)
        dma("S" if name in on_s else "Y", sig, waits, out, in_)

    def ts(sig, waits, out, in0, s1, o0, s2=None, o1=None):
        if o1 is None:
            add("V", sig, waits, lambda: V.tensor_scalar(out, in0, s1, None, o0))
        else:
            add("V", sig, waits, lambda: V.tensor_scalar(out, in0, s1, s2, o0, o1))

    def tt(sig, waits, out, in0, in1, o):
        add("V", sig, waits, lambda: V.tensor_tensor(out, in0, in1, o))

    def scan(sig, waits, out, d0, d1, init, o0, o1):
        add("V", sig, waits, lambda: V.tensor_tensor_scan(out, d0, d1, init, o0, o1))

    def fill(sig, waits, out, c):
        add("V", sig, waits, lambda: V.memset(out, c))

    def copy(q, sig, waits, out, in_):
        if q == "V":
            add(q, sig, waits, lambda: V.tensor_copy(out, in_))
        else:
            add(q, sig, waits, lambda: S.activation(out, in_, act.Copy))

    def affine(sig, waits, out, in_, scale, bias):
        if who() == "S":
            add("S", sig, waits, lambda: S.activation(out, in_, act.Identity, bias=bias, scale=scale))
        else:
            ts(sig, waits, out, in_, scale, op.mult, bias, op.add)

    def sign(sig, waits, out, in_):
        if who() == "S":
            add("S", sig, waits, lambda: S.activation(out, in_, act.Sign, bias=2.0 ** -120, scale=2.0 ** 16))
        else:
            ts(sig, waits, out, in_, 0.0, op.is_lt, -2.0, op.mult)

    def mm(sig, waits, terms, start=True, stop=True):
        for i, (out, lhs, rhs) in enumerate(terms):
            last = i == len(terms) - 1
            add("P", sig if last else None, waits if i == 0 else [],
                lambda out=out, lhs=lhs, rhs=rhs, a=start and i == 0, b=stop and last: P.matmul(out, lhs, rhs, a, b))

    def iota(sig, out, pattern, base, cm):
        add("G", sig, [], lambda: g.iota(out, pattern, base, cm, allow_small_or_imprecise_dtypes=True))

    def pick(sig, waits, out, in_, pattern, cmp, val, base, cm):
        add("G", sig, waits, lambda: g.affine_select(out, in_, pattern, cmp, val, base, cm))

    def levels(c0, n):
        return T.lvw[:, 0:NV].indirect(T.off[:, c0:c0 + n])

    def channels(c0):
        return T.chw[:, 0:PAD + NV].indirect(T.oabu[:, c0:c0 + XW])

    load("cor", "d_cor", [], T.lc[:], T.cor[:])
    load("bl", "d_bl", [], T.lst[:, 192:224], T.bl[:])
    load("kd0", "d_kd", [], T.kdx[:, 0:16], T.kd[0::2, :])
    load("kd1", "d_kd", [], T.kdx[:, 16:32], T.kd[1::2, :])
    load("lv", "d_lv", ["lvz"], T.lvw[0::16, :], T.lv[:])
    load("ea", "d_l", [], T.lst[:, 0:96], T.ea[:])
    load("eb", "d_l", [], T.lst[:, 96:192], T.eb[:])
    load("ce0", "d_ce", [], T.cex[:, 0], T.ce[0::2, :])
    load("ce1", "d_ce", [], T.cex[:, 1], T.ce[1::2, :])
    load("ch", "d_ch", ["lvz"], T.chw[:, PAD:PAD + NV], T.ch[:])
    for k in range(8):
        load("tab", "d_tab", [], T.tabw[16 * k:16 * k + 16, :], T.tab[:])

    diag, blocks = [[1, 128]], [[16, 8], [0, 16]]
    zer = T.zer[:, 0:128]
    part("zer")
    idb = T.idw[:, 16:144]
    iota("zer", T.zer[:], [[0, 160]], 0, 0)
    part("idb")
    pick("c_id", ["zer"], T.idw[:], T.zer[:], [[1, 160]], op.not_equal, 1.0, -16, -1)
    part("idh")
    pick("c_idh", ["zer"], T.idh[:], zer, diag, op.not_equal, 1.0, 0, -1)
    part("park")
    iota("i_park", T.park[:], [[16, 32]], A, 1)
    part("wd")
    pick("c_wd0", ["zer"], T.wd[:, 0], T.zer[:, 0:144], [[16, 9], [-200, 16]], op.not_equal, -0.5, 3000, -1)
    part("wc")
    pick("c_wc", ["zer"], T.wc[:], T.zer[:, 0:144], [[16, 9], [-200, 16]], op.not_equal, 1.0, 3012, -1)
    part("tri")
    pick("t1", ["zer"], T.t1[:], zer, [[-16, 8], [0, 16]], op.is_gt, 1.0, -15, 1)
    pick("c_tri", [], T.bi[:], zer, diag, op.not_equal, BIG, 0, -1)
    pick("blk", ["t1"], T.blk[:], T.t1[:], [[-16, 8], [0, 16]], op.is_ge, 0.0, 0, 1)
    part("tri2")
    pick("c_tri", ["blk"], T.low[:], T.blk[:], diag, op.is_gt, 0.0, 0, -1)
    pick("c_tri", [], T.upp[:], T.blk[:], [[-1, 128]], op.is_gt, 0.0, 0, 1)
    part("swap")
    pick("c_sw", ["c_id"], T.sw[:, 0], T.idw[:], [[0, 5], [1, 2], [0, 16]], op.is_gt, 0.0, 0, 0)
    pick("c_sw", [], T.sw[:, 1], T.idw[:], [[0, 5], [-1, 2], [0, 16]], op.is_gt, 0.0, 1, 0)
    part("b")
    pick("c_b", ["zer"], T.bc[:], zer, blocks, op.not_equal, 1.0, 0, -1)
    pick("c_b", [], T.nbc[:], zer, blocks, op.not_equal, -1.0, 0, -1)
    part("sel")
    pick("c_sel0", ["zer"], T.sel[:, 0], zer, blocks, op.not_equal, 1.0, 0, -1)
    dma("Y", "d_sel0", ["c_sel0"], T.seld[16:144, :], T.sel[:, 0])
    dma("Y", "d_sel0", [], T.seld[1:16, :], T.sel[1:16, 0])
    for a in range(1, 12):
        dma("Y", "d_sel", ["d_sel0"], T.sel[:, a], T.seld[16 - a:144 - a, :])
    part("r")
    w0 = 12 * BANKS[0]
    iota("i_r", T.rr[:, 0:w0], [[0, BANKS[0]], [-8192, 12]], 5 * 8192, 0)
    pick("c_r0", ["i_r"], T.rr[:, 0:w0:12], T.rr[:, 0:w0:12], [[0, BANKS[0]]], op.is_gt, 2.0 ** 21, 0, 0)
    for b in (1, 2):
        dma("Y", "d_r", ["c_r0"], T.rr[:, b * w0:b * w0 + 12 * BANKS[b]], T.rr[:, 0:12 * BANKS[b]])
    part("w")
    for k in range(6):
        affine("c_w", ["c_id"], T.w[:, k], idb, -BIG * (2 * k + 1), 0.0)
    part("wds")
    for kp in range(1, 4):
        affine("c_wd", ["c_wd0"], T.wd[:, kp], T.wd[:, 0], 2.0 ** kp, 0.0)

    lift = sum(0.5 * 2 ** (4 * kk + kp) for kk in range(2) for kp in range(4) if "c%d0%d" % (kk, kp // 2) in on_s)
    part("consts")
    fill("lvz", [], T.lvw[:], 0.0)
    fill("c_pat", [], T.pat[:, 0::2], 0.0)
    fill("c_pat", [], T.pat[:, 1::2], 16.0)
    fill("c_lift", [], T.lift[:, 0::2], 0.0)
    fill("c_lift", [], T.lift[:, 1::2], lift)
    fill("c_chz", [], T.chw[:, 0:PAD], 0.0)
    fill("vt", [], T.vt[:, Z:Z + 16], 0.0)
    fill("vt", [], T.vt[:, E + B * r:E + B * r + B], 0.0)
    fill("c_vw", [], T.vw[:, 0:A], float(Z))
    copy("V", "c_cey", ["zer"], T.cey[:, :, 12:16], zer)
    part("o_cor")
    for kk in range(2):
        for h in range(2):
            copy("V", "o_cor%d" % kk, ["d_cor"], T.off[:, 128 * kk + 64 * h:128 * kk + 64 * h + 64], T.lc[:, kk, :, h, :])
    part("o_l")
    copy("V", "o_l", ["d_l", "d_bl"], T.off[:, 256:480], T.lst[:])
    part("abf")
    ts("abf", ["d_l"], T.abf[:], T.lst[:, 0:192], -1024.0, op.add)
    part("kd")
    ts("kdb", ["d_kd"], T.kdb[:], T.kdx[:], 256.0, op.mult)

    for j in range(2):
        for kk in range(2):
            for h in range(2):
                part("c%d%d%d" % (kk, h, j))
                assert (who() == "S") == ("c%d0%d" % (kk, j) in on_s)
                p0 = 2048 * j + 2 * h + 1 - kk
                sign("g_c%d" % j, ["d_lv", "o_cor%d" % kk], T.gk[:, p0:2048 * (j + 1):4], levels(128 * kk + 64 * h + 32 * j, 32))
        part("c%d" % j)
        terms = [(T.pc[:, 0:64], T.wd[:, kp, 15 - t:143 - t], T.gk[:, 1024 * kp + 64 * t:1024 * kp + 64 * t + 64])
                 for kp in (2 * j, 2 * j + 1) for t in range(16)]
        if j == 0:
            mm(None, ["c_id", "c_lift"], [(T.pc[:, 0:64], idb, T.lift[:])], stop=False)
        mm("p_c" if j else None, ["g_c%d" % j, "c_wd0", "c_wd"], terms, start=False, stop=j == 1)

    part("snd_s")
    sign("snd", ["o_l", "d_lv"], T.sendb[:, 1::2], levels(448, 32))
    part("snd_c")
    copy(who(), "snd", ["o_l", "d_ch"], T.sendb[:, 0::2], T.chw[:, PAD:PAD + NV].indirect(T.off[:, 448:480]))
    part("send")
    sent = 0
    for call in exchange_calls(core, T, topo):
        trs = []
        for c, es in call:
            rid, pid = topo.addr(c, core)
            q = T.rank_of(c)
            trs.append(RemoteDMATransfer(dst_ids=[DstId(rid=rid, pnc=pid)], dma_engine_mask=sum(1 << e for e in es),
                                         remote_sem=T.sem.arr, src=T.sendb[:, 2 * B * q:2 * B * (q + 1)],
                                         dst=T.land[:, 2 * B * r:2 * B * (r + 1)]))
            sent += len(es)
        add("G", None, ["snd"], lambda trs=trs: g.remote_dma_fused(trs, local_sem=T.sem.sent))
    arrive = sum(len(es) for c0 in T.cores if c0 != core for call in exchange_calls(c0, T, topo) for c, es in call if c == core)
    part("end")
    add("G", None, ["sent"], None)

    part("case")
    scan("cs", ["p_c", "c_pat"], T.cs[:], T.pat[:], T.pc[:, 0:64], 0.0, op.mult, op.add)
    case = T.cs[:, 1::2]
    part("act0")
    ts("y255", ["cs"], T.y255[:], case, 0.5, op.is_gt, 255.0, op.mult)
    part("act1")
    tt("a", ["y255"], T.aa[:], case, T.y255[:], op.not_equal)
    part("l")
    a0, a1, pl = T.aa[:, 0::2], T.aa[:, 1::2], 128
    mm("p_l", ["a", "c_tri", "c_w", "c_id"], [(T.pc[:, pl:pl + 16], T.low[:], a0)])
    mm("p_l", [], [(T.pc[:, pl + 32:pl + 48], T.upp[:], a0), (T.pc[:, pl + 32:pl + 33], T.bi[:], T.aa[:, 30:31]),
                   (T.pc[:, pl + 32:pl + 48], T.low[:], a1)])
    for h in range(2):
        o = pl + 16 + 32 * h
        mm("p_l", [], [(T.pc[:, o:o + 16], idb, T.aa[:, h::2]), (T.pc[:, o + 1:o + 16], T.bi[:], T.aa[:, h:30:2]),
                       (T.pc[:, o:o + 16], T.w[:, 0], T.aa[:, h::2])])
    part("slot0")
    scan("lf", ["p_l", "zer"], T.lf[:], T.zer[:, 0:64], T.pc[:, pl:pl + 64], BIG - 1, op.add, op.add)
    part("slot1")
    for h in range(2):
        tt("lm", ["lf", "i_park"], T.lm[:, h::2], T.lf[:, 16 + 32 * h:32 + 32 * h], T.park[:, h::2], op.min)
    part("slot2")
    copy("V", "su", ["lm"], T.su[:], T.lm[:])

    part("cey")
    for k in range(2):
        copy("V", "cey", ["d_ce"], T.cey[:, k::2, 0:12], T.cex[:, k])
    part("sw")
    for k in range(2):
        out = T.pw[:, k:32:2]
        mm("p_sw", ["cs", "kdb", "c_sw", "c_id"],
           [(out, idb, T.kdb[:, 16 * k:16 * k + 16])]
           + [(out, T.sw[:, k, 16 * (1 + k - h):16 * (1 + k - h) + 128], T.cs[:, 1 + 2 * h::4]) for h in range(2)])
    part("col")
    copy("V", "cey", ["p_sw", "c_cey"], T.cey[:, :, 12], T.pw[:, 0:32])
    part("cez")
    add("V", "cez", ["cey"], lambda: V.transpose(T.cez[:], T.cey[:]))
    part("scat")
    copy("V", "vw", ["su", "cez", "c_vw"], T.vw[:, 0:768].indirect(T.su[:, 0:32]), T.cez[:])
    part("vh")
    copy("V", "vh", ["vw"], T.vh[:], T.vw[:, 0:A])
    part("cw")
    mm("p_cw", ["vh", "c_wc"], [(T.pw[:, 64:71], T.wc[:, 15 - t:143 - t], T.vh[:, t::16]) for t in range(16)])
    part("colu")
    ts("colu", ["p_cw"], T.colu[:, 0:7], T.pw[:, 64:71], 2047.0, op.min)
    part("tabg")
    affine("xp", ["colu", "d_tab"], T.xp[:], T.tabw[:, 0:2048].indirect(T.colu[:, 0:7]), 1.0, -5.5)
    part("xn")
    affine("xn", ["xp"], T.xn[:], T.xp[:], -1.0, 0.0)
    part("xq")
    add("S", "xq", ["xp", "d_r"], lambda: S.activation(T.rr[:, 11::12], T.xp[:], act.Square, scale=64.0))

    m0 = 0
    for b, n in enumerate(BANKS):
        pd, sl = T["pe%d" % b], slice(m0, m0 + n)
        order = [(j, (j + 1) % 12) for j in range(12)]
        part("d%d" % b)
        mm(None, ["zer", "d_lv"] + ["oabu%d" % c for c in range(EC) if c == b],
           [(pd[:, 0:12 * n], zer, T.lvw[:, 0:12 * n])], stop=False)
        part("dc%d" % b)
        mm(None, ["vh", "d_sel"], [(pd[:, j:12 * n:12], T.sel[:, a], T.vh[:, sl]) for j, a in order], start=False, stop=False)
        part("dx%d" % b)
        for j, a in sorted(order, key=lambda ja: -ja[1]):
            x = "xp" if a > 5 else "xn"
            mm("p_d%d" % b, [x], [(pd[:, j:12 * n:12], T.w[:, abs(2 * a - 11) // 2], T[x][:, sl])], start=False, stop=False)
        mm("p_d%d" % b, ["xq"], [(pd[:, 11:12 * n:12], idb, T.rr[:, 12 * m0 + 11:12 * (m0 + n):12])], start=False)
        part("sel%d" % b)
        scan("sc%d" % b, ["p_d%d" % b], T.sc[:, 12 * m0:12 * (m0 + n)], T.rr[:, 12 * m0:12 * (m0 + n)], pd[:, 0:12 * n],
             0.0, op.add, op.min)
        part("eu%d" % b)
        ts("eu%d" % b, ["sc%d" % b], T.eu[:, sl], T.sc[:, 12 * m0 + 11:12 * (m0 + n):12], 121 * 1024.0, op.add, float(Z), op.min)
        m0 += n

    for c in range(EC):
        n = "%d" % c
        pe = T["pe" + n]
        a0, b0, e0 = 2 * EW * c, 2 * EW * c + EW, EW * c
        low = 0.0
        for h in range(2):
            part("e%s%s" % ("ab"[h], n))
            low += 0.5 * (who() == "S")
            c0 = a0 + EW * h
            sign("g_" + here[0], ["o_l", "d_lv"], T.ge[:, 16 * c0:16 * (c0 + EW)], levels(256 + 96 * h + e0, EW))
            mm("p_e" + n if h else None, ["g_" + here[0], "c_wd0"],
               [(pe[:, 0:EW], T.wd[:, 0, 15 - t:143 - t], T.ge[:, 16 * c0 + t:16 * (c0 + EW):16]) for t in range(16)],
               start=h == 0, stop=h == 1)
        part("se" + n)
        se = T.se[:, e0:e0 + EW]
        if who() == "S":
            add("S", "se" + n, ["p_e" + n], lambda se=se, pe=pe, low=low: S.activation(se, pe[:, 0:EW], act.Abs, bias=low - 1.0))
        else:
            ts("se" + n, ["p_e" + n], se, pe[:, 0:EW], 1.0 - low, op.not_equal)
        part("x" + n)
        for h in range(2):
            out = pe[:, 256 + EW * h:256 + EW * (h + 1)]
            mm("p_x" + n, ["se" + n, "abf", "c_idh", "c_w"],
               [(out, T.idh[:], T.abf[:, 96 * h + e0:96 * h + e0 + EW]), (out, T.w[:, 0], se)])
        part("z" + n)
        ts("oabu" + n, ["p_x" + n], T.oabu[:, a0:a0 + 2 * EW], pe[:, 256:256 + 2 * EW], 1024.0 + PAD, op.add)
    done = ["vt"]
    for i in range(96 // XW):
        n, c, e0 = "%d" % i, XW * i // EW, XW * i
        a0, cols = e0 + EW * c, slice(16 * e0, 16 * (e0 + XW))
        part("xa" + n)
        copy(who(), "xa" + n, ["oabu%d" % c, "d_ch", "c_chz"], T.xa[:, cols], channels(a0))
        part("xb" + n)
        if who() == "V":
            tt("vt", ["xa" + n], T.vt[:, cols], channels(a0 + EW), T.xa[:, cols], op.add)
        else:
            copy("S", "xs" + n, ["oabu%d" % c, "d_ch", "c_chz"], T.xs[:, cols], channels(a0 + EW))
            part("s" + n)
            out = T.ps[:, 0:16 * XW]
            mm("p_s" + n, ["xa" + n, "xs" + n, "c_id"] + done[1:], [(out, idb, T.xa[:, cols]), (out, idb, T.xs[:, cols])])
            copy("S", "vt" + n, ["p_s" + n], T.vt[:, cols], out)
            done.append("vt" + n)

    spans = [(a, b) for a, b in ((0, B * r), (B * r + B, B * N)) if b > a]
    part("b")
    for a, b in spans:
        mm("p_bd", ["snd", "c_b", "arr"], [(T.pbd[:, a:b], T.bc[:], T.sendb[:, 2 * a + 1:2 * b:2]),
                                           (T.pbd[:, a:b], T.nbc[:], T.land[:, 2 * a + 1:2 * b:2])])
    for a, b in spans:
        mm("p_bs", ["c_id"], [(T.pbs[:, a:b], idb, T.sendb[:, 2 * a:2 * b:2]), (T.pbs[:, a:b], idb, T.land[:, 2 * a:2 * b:2])])
    part("cb")
    for a, b in spans:
        add("S", "cb", ["p_bd"], lambda a=a, b=b: S.activation(T.cb[:, a:b], T.pbd[:, a:b], act.Abs, scale=0.5))
    part("vb")
    for a, b in spans:
        tt("vt", ["cb", "p_bs"], T.vt[:, E + a:E + b], T.pbs[:, a:b], T.cb[:, a:b], op.mult)

    m0 = 0
    for i, n in enumerate(CFG["out"]):
        need = ["eu%d" % b for b in range(3) if sum(BANKS[:b]) < m0 + n and m0 < sum(BANKS[:b + 1])]
        yo = T.yo[:, 16 * m0:16 * (m0 + n)]
        part("y%d" % i)
        copy(who(), "y%d" % i, done + need, yo, T.vt[:, 0:Z + 16].indirect(T.eu[:, m0:m0 + n]))
        dma("Y", "d_y", ["y%d" % i], T.y[:, 16 * m0:16 * (m0 + n)], yo)
        m0 += n
    part("out")
    add("Y", None, ["d_y"], None)

    emit(eng, parts, T, {"arr": arrive, "sent": sent})


def emit(eng, parts, T, outside):
    prog = {}
    for q in eng:
        names = CFG[q].split()
        assert sorted(names) == sorted(parts[q]), (q, set(names) ^ set(parts[q]))
        prog[q] = [x for name in names for x in parts[q][name]]
    total, left = dict(outside), {}
    for q in prog:
        for sig, waits, fn, inc in prog[q]:
            if sig:
                total[sig] = total.get(sig, 0) + inc
                left[sig] = left.get(sig, 0) + 1
    known = {q: set() for q in prog}
    carry = {}
    pos = {q: 0 for q in prog}
    order, used = [], set()
    moved = True
    while moved:
        moved = False
        for q in prog:
            while pos[q] < len(prog[q]):
                sig, waits, fn, inc = prog[q][pos[q]]
                if any(left.get(w, 0) for w in waits):
                    break
                need = [w for w in waits if w not in known[q]]
                need = [w for w in need if not any(w in carry.get(v, ()) for v in need if v != w)]
                for w in need:
                    known[q].add(w)
                    known[q] |= carry.get(w, set())
                used.update(need)
                if sig:
                    carry.setdefault(sig, set()).update(known[q])
                    left[sig] -= 1
                order.append((q, sig, need, fn, inc))
                pos[q] += 1
                moved = True
    assert all(pos[q] == len(prog[q]) for q in prog), [(q, prog[q][pos[q]][:2]) for q in prog if pos[q] < len(prog[q])]
    names = {k: k for k in outside}
    for q, sig, need, fn, inc in order:
        if sig in used and sig not in names:
            names[sig] = "s%d" % (len(names) - len(outside))
    for q, sig, need, fn, inc in order:
        for w in need:
            eng[q].wait_ge(T.sem[names[w]], total[w])
        if fn is not None:
            ins = fn()
            if sig in used:
                ins.then_inc(T.sem[names[sig]], inc)
